import numpy as np
import ml_dtypes


def mxq(x, axis, fmt="e4m3"):
    dtype, down = {"e4m3": (ml_dtypes.float8_e4m3fn, 7), "e5m2": (ml_dtypes.float8_e5m2, 14)}[fmt]
    v = np.moveaxis(np.asarray(x, np.float32).astype(ml_dtypes.bfloat16).astype(np.float64), axis, -1)
    blocks = v.reshape(v.shape[:-1] + (-1, 32))
    amax = np.abs(blocks).max(-1, keepdims=True)
    byte = np.maximum(np.where(amax > 0, np.frexp(amax)[1] - 1 + 127, 0) - down, 1)
    scale = np.exp2(byte - 127.0)
    codes = (blocks / scale).astype(np.float32).astype(dtype).astype(np.float64)
    return np.moveaxis((codes * scale).reshape(v.shape), -1, axis)


WIDE = False


def mx_kscale(k):
    if not WIDE:
        return np.ones(k)
    levels = np.array([10, -10, 5, -5, 0])
    if k % 512:
        return np.exp2(np.random.permutation(np.resize(levels, k // 32))).repeat(32)
    a = np.empty((k // 512, 16))
    for p in range(k // 512):
        a[p, :8] = np.random.permutation(np.resize(levels, 8))
        for g in range(8):
            far = levels[np.abs(levels - a[p, g]) >= 10]
            a[p, g + 8] = far[np.random.randint(len(far))]
    return np.exp2(a.ravel()).repeat(32)


def f64(x):
    return np.asarray(x).astype(np.float64)


def striped(idx):
    return np.tile(idx.reshape(-1, 16).T, (8, 1)).astype(np.uint16)


def unstriped(offs):
    return offs[:16].T.reshape(-1).astype(np.int64)


def striped8(idx):
    return np.concatenate([x.reshape(-1, 16).T for x in idx]).astype(np.uint16)


def runs(offs, k):
    lists = np.stack([offs[16 * r : 16 * r + 16].T.reshape(-1) for r in range(8)]).astype(np.int64)
    return lists[np.arange(k) % 512 // 64]


def pack_weight(w):
    k, n = w.shape
    w = f64(np.asarray(w, np.float32).astype(ml_dtypes.bfloat16)).reshape(k // 32, 32, n)
    amax = np.abs(w).max(1)
    byte = np.clip(np.where(amax > 0, np.frexp(amax)[1] - 1 + 127 - 7, 1), 1, 254)
    scaled = (w * np.exp2(127.0 - byte)[:, None, :]).reshape(k, n).astype(np.float32)
    words = np.ascontiguousarray(scaled.reshape(k // 512, 128, 4, n).transpose(0, 1, 3, 2)).astype(ml_dtypes.float8_e4m3fn).view(np.uint8)
    return words, np.ascontiguousarray(byte.astype(np.uint8).reshape(k // 512, 16, n))


def unpack_weight(words, scales):
    g, p, n, _ = words.shape
    vals = np.ascontiguousarray(words).view(ml_dtypes.float8_e4m3fn).astype(np.float64) * np.repeat(np.exp2(scales.astype(np.float64) - 127.0), 8, axis=1)[..., None]
    return vals.transpose(0, 1, 3, 2).reshape(g * 512, n)


K, T, S, N, H = 512, 2048, 512, 512, 512


def setup_inputs():
    n = np.random.standard_normal
    s = mx_kscale(K)[:, None]
    u = mx_kscale(H)
    packed_xT = pack_weight(n((K, T)) * s)
    return {
        "x_words": packed_xT[0],
        "x_scales": packed_xT[1],
        "w1": (n((K, H)) / np.sqrt(K) / s).astype(np.float32),
        "gn": (np.random.uniform(0.5, 1.5, (H, 1)) * u[:, None]).astype(np.float32),
        "w2": (n((H, N)) / np.sqrt(H) / u[:, None]).astype(np.float32),
        "offs": striped(np.random.permutation(T)[:S]),
        "n1": striped8(np.stack([np.random.permutation(S) for _ in range(8)])),
        "n2": striped8(np.stack([np.random.permutation(S) for _ in range(8)])),
        "n3": striped8(np.stack([np.random.permutation(S) for _ in range(8)])),
    }


def reference(x_words, x_scales, w1, gn, w2, offs, n1, n2, n3):
    xq = unpack_weight(x_words, x_scales)[:, unstriped(offs)]
    y = mxq(f64(w1), 0, "e4m3").T @ xq
    z = f64(gn) * (np.maximum(y, y[np.arange(H)[:, None], runs(n1, H)]))
    h = mxq(f64(w2), 0, "e4m3").T @ mxq(z, 0, "e4m3")
    return h[np.arange(N)[:, None], runs(n2, N)] - (np.tanh(y) * (y[np.arange(H)[:, None], runs(n3, H)]))

@@ -1,0 +1,169 @@
+from contextlib import ExitStack
+
+import concourse.mybir as mybir
+
+F32 = mybir.dt.float32
+BF16 = mybir.dt.bfloat16
+I32 = mybir.dt.int32
+U32 = mybir.dt.uint32
+U16 = mybir.dt.uint16
+U8 = mybir.dt.uint8
+FP8X4 = mybir.dt.float8_e4m3fn_x4
+ALU = mybir.AluOpType
+ACT = mybir.ActivationFunctionType
+
+P = 128
+PACK = 4
+T, S, C = 2048, 512, 512
+HALF = S // 2
+WINDOW = 2 * S
+M_SCALAR = 48
+FLOPS = 2 * 2 * 512 * 512 * 512
+
+
+def deal_views(grouped, raw, m0, m1):
+    dst = grouped[:].rearrange("p (t m j) -> p m j t", t=PACK, j=PACK)[:, m0:m1]
+    src = raw[:].rearrange("p j (m t) -> p m j t", t=PACK)[:, m0:m1]
+    return dst, src
+
+
+def tile_picked_skipsoftbbig_none_p_kernel(tc, x_words, x_scales, w1, gn, w2, offs, n1, n2, n3, out):
+    nc = tc.nc
+    with ExitStack() as ctx:
+        lists = ctx.enter_context(tc.tile_pool(name="lists", bufs=1))
+        sb = ctx.enter_context(tc.tile_pool(name="sb", bufs=1))
+        psum = ctx.enter_context(tc.psum_pool(name="psum", bufs=1))
+
+        offs_sb = lists.tile([P, S // 16], U16, name="offs_sb")
+        n1_sb = lists.tile([P, S // 16], U16, name="n1_sb")
+        n2_sb = lists.tile([P, S // 16], U16, name="n2_sb")
+        n3_sb = lists.tile([P, S // 16], U16, name="n3_sb")
+
+        xw = sb.tile([P, T], U32, name="xw", align_bytes=64)
+        xs = sb.tile([P, T], U8, name="xs", align_bytes=64)
+        w1_raw = sb.tile([P, PACK, C], F32, name="w1_raw", align_bytes=64)
+        w2_raw = sb.tile([P, PACK, C], F32, name="w2_raw", align_bytes=64)
+        gn_sb = sb.tile([P, PACK], F32, name="gn_sb")
+        y = [sb.tile([P, WINDOW], F32, name="y%d" % t, align_bytes=64) for t in range(PACK)]
+        h = [sb.tile([P, WINDOW], F32, name="h%d" % t, align_bytes=64) for t in range(PACK)]
+
+        nc.vector.memset(xs[:].bitcast(I32), 0)
+        nc.sync.dma_start(offs_sb[:], offs)
+        nc.sync.dma_start(out=w1_raw[:], in_=w1.rearrange("(p j) c -> p j c", j=PACK))
+        for q in range(4):
+            nc.scalar.dma_start(out=xs[32 * q : 32 * q + 4, :].bitcast(I32), in_=x_scales[0, 4 * q : 4 * q + 4, :].bitcast(I32))
+        nc.sync.dma_start(out=xw[:].bitcast(I32), in_=x_words[0].rearrange("p n t -> p (n t)").bitcast(I32))
+        nc.sync.dma_start(n1_sb[:], n1)
+        nc.sync.dma_start(out=w2_raw[:], in_=w2.rearrange("(p j) c -> p j c", j=PACK))
+        nc.sync.dma_start(n3_sb[:], n3)
+        nc.sync.dma_start(n2_sb[:], n2)
+        nc.gpsimd.dma_start(out=gn_sb[:], in_=gn.rearrange("(p t) o -> p (t o)", t=PACK))
+        for t in range(PACK):
+            nc.vector.memset(y[t][:, S:], 0.0)
+            nc.gpsimd.memset(h[t][:, S:], 0.0)
+
+        gs = sb.tile([P, S], U8, name="gs", align_bytes=64)
+        nc.vector.tensor_copy(out=gs[:], in_=xs[:].indirect(offs_sb[:]))
+
+        w1_bf = sb.tile([P, PACK * C], BF16, name="w1_bf", align_bytes=64)
+        dst, src = deal_views(w1_bf, w1_raw, 0, M_SCALAR)
+        nc.scalar.copy(out=dst, in_=src)
+        dst, src = deal_views(w1_bf, w1_raw, M_SCALAR, P)
+        nc.vector.tensor_copy(out=dst, in_=src)
+        w1_codes = sb.tile([P, C], U32, name="w1_codes", align_bytes=64)
+        w1_scales = sb.tile([P, C], U8, name="w1_scales", align_bytes=64)
+        nc.vector.quantize_mx(out=w1_codes[:].bitcast(FP8X4), scales=w1_scales[:], in_=w1_bf[:])
+
+        gw = [sb.tile([P, HALF], U32, name="gw%d" % a, align_bytes=64) for a in range(2)]
+        for a in range(2):
+            nc.vector.tensor_copy(out=gw[a][:], in_=xw[:].indirect(offs_sb[:, 16 * a : 16 * (a + 1)]))
+
+        y_ps = {}
+        for pair in range(2):
+            for a in range(2):
+                for t in (2 * pair, 2 * pair + 1):
+                    acc = psum.tile([P, HALF], F32, name="y_ps", tag="bank%d" % (2 * t + a))
+                    nc.tensor.matmul_mx(
+                        out=acc[:],
+                        lhsT=w1_codes[:, P * t : P * (t + 1)].bitcast(FP8X4),
+                        lhsT_scale=w1_scales[:, P * t : P * (t + 1)],
+                        rhs=gw[a][:].bitcast(FP8X4),
+                        rhs_scale=gs[:, HALF * a : HALF * (a + 1)],
+                        start=True,
+                        stop=True,
+                    )
+                    y_ps[(t, a)] = acc
+
+        th = [sb.tile([P, S], F32, name="th%d" % t) for t in range(PACK)]
+        nc.scalar.activation(out=th[0][:, :HALF], in_=y_ps[(0, 0)][:], func=ACT.Tanh)
+        for t in range(PACK):
+            for a in range(2):
+                nc.scalar.copy(out=y[t][:, HALF * a : HALF * (a + 1)], in_=y_ps[(t, a)][:])
+
+        w2_bf = sb.tile([P, PACK * C], BF16, name="w2_bf", align_bytes=64)
+        dst, src = deal_views(w2_bf, w2_raw, 0, P)
+        nc.scalar.copy(out=dst, in_=src)
+
+        g = [sb.tile([P, S], F32, name="g%d" % t) for t in range(PACK)]
+        mx = [sb.tile([P, S], F32, name="mx%d" % t) for t in range(PACK)]
+        z_planes = sb.tile([P, PACK, S], BF16, name="z_planes", align_bytes=64)
+
+        def fetch(t):
+            nc.vector.tensor_copy(out=g[t][:], in_=y[t][:].indirect(n1_sb[:]))
+
+        def larger(t):
+            nc.vector.tensor_tensor(out=mx[t][:], in0=g[t][:], in1=y[t][:, :S], op=ALU.max)
+            nc.scalar.activation(out=z_planes[:, t, :], in_=mx[t][:], func=ACT.Copy, scale=gn_sb[:, t : t + 1])
+
+        fetch(0)
+        fetch(1)
+        larger(0)
+        fetch(2)
+        larger(1)
+        nc.scalar.activation(out=th[0][:, HALF:], in_=y[0][:, HALF:S], func=ACT.Tanh)
+        nc.scalar.activation(out=th[1][:], in_=y[1][:, :S], func=ACT.Tanh)
+        fetch(3)
+        larger(2)
+        larger(3)
+
+        z_bf = sb.tile([P, PACK * S], BF16, name="z_bf", align_bytes=64)
+        nc.scalar.copy(
+            out=z_bf[:].rearrange("p (c i t) -> p c t i", i=4, t=PACK),
+            in_=z_planes[:].rearrange("p t (c i) -> p c t i", i=4),
+        )
+        for t in (2, 3):
+            nc.scalar.activation(out=th[t][:], in_=y[t][:, :S], func=ACT.Tanh)
+
+        prod = [sb.tile([P, S], F32, name="prod%d" % t) for t in range(PACK)]
+
+        def product(t):
+            nc.vector.tensor_tensor(out=prod[t][:], in0=y[t][:].indirect(n3_sb[:]), in1=th[t][:], op=ALU.mult)
+
+        product(0)
+        product(1)
+        w2_codes = sb.tile([P, C], U32, name="w2_codes", align_bytes=64)
+        w2_scales = sb.tile([P, C], U8, name="w2_scales", align_bytes=64)
+        nc.vector.quantize_mx(out=w2_codes[:].bitcast(FP8X4), scales=w2_scales[:], in_=w2_bf[:])
+        z_codes = sb.tile([P, S], U32, name="z_codes", align_bytes=64)
+        z_scales = sb.tile([P, S], U8, name="z_scales", align_bytes=64)
+        nc.vector.quantize_mx(out=z_codes[:].bitcast(FP8X4), scales=z_scales[:], in_=z_bf[:])
+        product(2)
+        product(3)
+
+        out_rows = out.rearrange("(p t) c -> p t c", t=PACK)
+        for t in range(PACK):
+            acc = psum.tile([P, S], F32, name="h_ps", tag="bank%d" % (2 * t))
+            nc.tensor.matmul_mx(
+                out=acc[:],
+                lhsT=w2_codes[:, P * t : P * (t + 1)].bitcast(FP8X4),
+                lhsT_scale=w2_scales[:, P * t : P * (t + 1)],
+                rhs=z_codes[:].bitcast(FP8X4),
+                rhs_scale=z_scales[:],
+                start=True,
+                stop=True,
+            )
+            nc.scalar.copy(out=h[t][:, :S], in_=acc[:])
+        for t in range(PACK):
+            res = sb.tile([P, S], F32, name="res%d" % t)
+            nc.vector.tensor_tensor(out=res[:], in0=h[t][:].indirect(n2_sb[:]), in1=prod[t][:], op=ALU.subtract)
+            nc.sync.dma_start(out=out_rows[:, t, :], in_=res[:])

@@ -14,17 +14,34 @@ ACT = mybir.ActivationFunctionType
 
 P = 128
 PACK = 4
-T, S, C = 2048, 512, 512
+T = 2048
+S = 512
+C = 512
+GROUP = 16
+QUADRANT = 32
 HALF = S // 2
 WINDOW = 2 * S
-M_SCALAR = 48
+FINE_EDGES = [0, HALF, HALF + P, S]
+W1_M_SCALAR = 72
 FLOPS = 2 * 2 * 512 * 512 * 512
 
 
-def deal_views(grouped, raw, m0, m1):
+def deal_views(grouped, raw, m0, m1, raw_m0):
     dst = grouped[:].rearrange("p (t m j) -> p m j t", t=PACK, j=PACK)[:, m0:m1]
-    src = raw[:].rearrange("p j (m t) -> p m j t", t=PACK)[:, m0:m1]
+    src = raw[:].rearrange("p j (m t) -> p m j t", t=PACK)[:, m0 - raw_m0 : m1 - raw_m0]
     return dst, src
+
+
+def product_tile(nc, acc, w_codes, w_scales, t, codes, scales):
+    nc.tensor.matmul_mx(
+        out=acc,
+        lhsT=w_codes[:, P * t : P * (t + 1)].bitcast(FP8X4),
+        lhsT_scale=w_scales[:, P * t : P * (t + 1)],
+        rhs=codes.bitcast(FP8X4),
+        rhs_scale=scales,
+        start=True,
+        stop=True,
+    )
 
 
 def tile_picked_skipsoftbbig_none_p_kernel(tc, x_words, x_scales, w1, gn, w2, offs, n1, n2, n3, out):
@@ -34,136 +51,134 @@ def tile_picked_skipsoftbbig_none_p_kernel(tc, x_words, x_scales, w1, gn, w2, of
         sb = ctx.enter_context(tc.tile_pool(name="sb", bufs=1))
         psum = ctx.enter_context(tc.psum_pool(name="psum", bufs=1))
 
-        offs_sb = lists.tile([P, S // 16], U16, name="offs_sb")
-        n1_sb = lists.tile([P, S // 16], U16, name="n1_sb")
-        n2_sb = lists.tile([P, S // 16], U16, name="n2_sb")
-        n3_sb = lists.tile([P, S // 16], U16, name="n3_sb")
+        offs_sb = lists.tile([P, S // GROUP], U16, name="offs_sb")
+        n1_sb = lists.tile([P, S // GROUP], U16, name="n1_sb")
+        n2_sb = lists.tile([P, S // GROUP], U16, name="n2_sb")
+        n3_sb = lists.tile([P, S // GROUP], U16, name="n3_sb")
 
         xw = sb.tile([P, T], U32, name="xw", align_bytes=64)
-        xs = sb.tile([P, T], U8, name="xs", align_bytes=64)
+        xs = sb.tile([P, T], U8, name="xs", tag="after_xs", align_bytes=64)
         w1_raw = sb.tile([P, PACK, C], F32, name="w1_raw", align_bytes=64)
-        w2_raw = sb.tile([P, PACK, C], F32, name="w2_raw", align_bytes=64)
+        w2_lo = sb.tile([P, PACK, C // 2], F32, name="w2_lo", align_bytes=64)
+        w2_hi = sb.tile([P, PACK, C // 2], F32, name="w2_hi", tag="after_w2_hi", align_bytes=64)
         gn_sb = sb.tile([P, PACK], F32, name="gn_sb")
         y = [sb.tile([P, WINDOW], F32, name="y%d" % t, align_bytes=64) for t in range(PACK)]
-        h = [sb.tile([P, WINDOW], F32, name="h%d" % t, align_bytes=64) for t in range(PACK)]
+        h = [sb.tile([P, S if t == PACK - 1 else WINDOW], F32, name="h%d" % t, align_bytes=64) for t in range(PACK)]
 
-        nc.vector.memset(xs[:].bitcast(I32), 0)
-        nc.sync.dma_start(offs_sb[:], offs)
+        nc.gpsimd.memset(xs[:, : T // 2].bitcast(I32), 0)
+        nc.vector.memset(xs[:, T // 2 :].bitcast(I32), 0)
+
         nc.sync.dma_start(out=w1_raw[:], in_=w1.rearrange("(p j) c -> p j c", j=PACK))
-        for q in range(4):
-            nc.scalar.dma_start(out=xs[32 * q : 32 * q + 4, :].bitcast(I32), in_=x_scales[0, 4 * q : 4 * q + 4, :].bitcast(I32))
-        nc.sync.dma_start(out=xw[:].bitcast(I32), in_=x_words[0].rearrange("p n t -> p (n t)").bitcast(I32))
+        nc.sync.dma_start(offs_sb[:], offs)
         nc.sync.dma_start(n1_sb[:], n1)
-        nc.sync.dma_start(out=w2_raw[:], in_=w2.rearrange("(p j) c -> p j c", j=PACK))
+        for q in range(P // QUADRANT):
+            nc.sync.dma_start(
+                out=xs[QUADRANT * q : QUADRANT * q + 4, :].bitcast(I32),
+                in_=x_scales[0, 4 * q : 4 * q + 4, :].bitcast(I32),
+            )
+        nc.sync.dma_start(out=xw[:].bitcast(I32), in_=x_words[0].rearrange("p n t -> p (n t)").bitcast(I32))
+        w2_rows = w2.rearrange("(p j) c -> p j c", j=PACK)
+        nc.sync.dma_start(out=w2_lo[:], in_=w2_rows[:, :, : C // 2])
+        nc.sync.dma_start(out=w2_hi[:], in_=w2_rows[:, :, C // 2 :])
         nc.sync.dma_start(n3_sb[:], n3)
         nc.sync.dma_start(n2_sb[:], n2)
-        nc.gpsimd.dma_start(out=gn_sb[:], in_=gn.rearrange("(p t) o -> p (t o)", t=PACK))
-        for t in range(PACK):
-            nc.vector.memset(y[t][:, S:], 0.0)
-            nc.gpsimd.memset(h[t][:, S:], 0.0)
+        nc.sync.dma_start(out=gn_sb[:], in_=gn.rearrange("(p t) o -> p (t o)", t=PACK))
 
-        gs = sb.tile([P, S], U8, name="gs", align_bytes=64)
+        gs = sb.tile([P, S], U8, name="gs", tag="after_gs", align_bytes=64)
         nc.vector.tensor_copy(out=gs[:], in_=xs[:].indirect(offs_sb[:]))
 
         w1_bf = sb.tile([P, PACK * C], BF16, name="w1_bf", align_bytes=64)
-        dst, src = deal_views(w1_bf, w1_raw, 0, M_SCALAR)
+        dst, src = deal_views(w1_bf, w1_raw, 0, W1_M_SCALAR, 0)
         nc.scalar.copy(out=dst, in_=src)
-        dst, src = deal_views(w1_bf, w1_raw, M_SCALAR, P)
+        dst, src = deal_views(w1_bf, w1_raw, W1_M_SCALAR, P, 0)
         nc.vector.tensor_copy(out=dst, in_=src)
-        w1_codes = sb.tile([P, C], U32, name="w1_codes", align_bytes=64)
-        w1_scales = sb.tile([P, C], U8, name="w1_scales", align_bytes=64)
+        w1_codes = sb.tile([P, C], U32, name="w1_codes", tag="after_xs", align_bytes=64)
+        w1_scales = sb.tile([P, C], U8, name="w1_scales", tag="after_w1_scales", align_bytes=64)
         nc.vector.quantize_mx(out=w1_codes[:].bitcast(FP8X4), scales=w1_scales[:], in_=w1_bf[:])
 
-        gw = [sb.tile([P, HALF], U32, name="gw%d" % a, align_bytes=64) for a in range(2)]
-        for a in range(2):
-            nc.vector.tensor_copy(out=gw[a][:], in_=xw[:].indirect(offs_sb[:, 16 * a : 16 * (a + 1)]))
-
-        y_ps = {}
-        for pair in range(2):
-            for a in range(2):
-                for t in (2 * pair, 2 * pair + 1):
-                    acc = psum.tile([P, HALF], F32, name="y_ps", tag="bank%d" % (2 * t + a))
-                    nc.tensor.matmul_mx(
-                        out=acc[:],
-                        lhsT=w1_codes[:, P * t : P * (t + 1)].bitcast(FP8X4),
-                        lhsT_scale=w1_scales[:, P * t : P * (t + 1)],
-                        rhs=gw[a][:].bitcast(FP8X4),
-                        rhs_scale=gs[:, HALF * a : HALF * (a + 1)],
-                        start=True,
-                        stop=True,
-                    )
-                    y_ps[(t, a)] = acc
-
-        th = [sb.tile([P, S], F32, name="th%d" % t) for t in range(PACK)]
-        nc.scalar.activation(out=th[0][:, :HALF], in_=y_ps[(0, 0)][:], func=ACT.Tanh)
-        for t in range(PACK):
-            for a in range(2):
-                nc.scalar.copy(out=y[t][:, HALF * a : HALF * (a + 1)], in_=y_ps[(t, a)][:])
+        gw = sb.tile([P, S], U32, name="gw", tag="after_gw", align_bytes=64)
+        for c0 in (0, HALF):
+            picks = offs_sb[:, c0 // GROUP : (c0 + HALF) // GROUP]
+            nc.vector.tensor_copy(out=gw[:, c0 : c0 + HALF], in_=xw[:].indirect(picks))
 
         w2_bf = sb.tile([P, PACK * C], BF16, name="w2_bf", align_bytes=64)
-        dst, src = deal_views(w2_bf, w2_raw, 0, P)
-        nc.scalar.copy(out=dst, in_=src)
+        dst, src = deal_views(w2_bf, w2_lo, 0, P // 2, 0)
+        nc.vector.tensor_copy(out=dst, in_=src)
 
-        g = [sb.tile([P, S], F32, name="g%d" % t) for t in range(PACK)]
-        mx = [sb.tile([P, S], F32, name="mx%d" % t) for t in range(PACK)]
-        z_planes = sb.tile([P, PACK, S], BF16, name="z_planes", align_bytes=64)
+        y_pieces = [(0, c0, c1) for c0, c1 in zip(FINE_EDGES[:-1], FINE_EDGES[1:])] + [(t, 0, S) for t in range(1, PACK)]
+        for bank, (t, c0, c1) in enumerate(y_pieces):
+            y_ps = psum.tile([P, c1 - c0], F32, name="y_ps", tag="bank%d" % bank)
+            product_tile(nc, y_ps[:], w1_codes, w1_scales, t, gw[:, c0:c1], gs[:, c0:c1])
+            nc.scalar.copy(out=y[t][:, c0:c1], in_=y_ps[:])
 
-        def fetch(t):
-            nc.vector.tensor_copy(out=g[t][:], in_=y[t][:].indirect(n1_sb[:]))
+        tanh_early = sb.tile([P, 2, S], F32, name="tanh_early", tag="after_gs", align_bytes=64)
+        tanh_y = [tanh_early[:, t, :] for t in range(2)]
+        for t in range(2):
+            nc.scalar.activation(out=tanh_y[t], in_=y[t][:, :S], func=ACT.Tanh)
 
-        def larger(t):
-            nc.vector.tensor_tensor(out=mx[t][:], in0=g[t][:], in1=y[t][:, :S], op=ALU.max)
-            nc.scalar.activation(out=z_planes[:, t, :], in_=mx[t][:], func=ACT.Copy, scale=gn_sb[:, t : t + 1])
+        for m0 in range(P // 2, P, P // 4):
+            dst, src = deal_views(w2_bf, w2_hi, m0, m0 + P // 4, P // 2)
+            nc.scalar.copy(out=dst, in_=src)
 
-        fetch(0)
-        fetch(1)
-        larger(0)
-        fetch(2)
-        larger(1)
-        nc.scalar.activation(out=th[0][:, HALF:], in_=y[0][:, HALF:S], func=ACT.Tanh)
-        nc.scalar.activation(out=th[1][:], in_=y[1][:, :S], func=ACT.Tanh)
-        fetch(3)
-        larger(2)
-        larger(3)
+        looked_up = [sb.tile([P, S], F32, name="looked_up%d" % t, align_bytes=64) for t in range(PACK)]
+        larger_tags = ["after_w1_scales", "after_xs", "after_gw", "after_larger3"]
+        larger = [sb.tile([P, S], F32, name="larger%d" % t, tag=larger_tags[t], align_bytes=64) for t in range(PACK)]
+        z_pairs = sb.tile([P, PACK * S], BF16, name="z_pairs", tag="after_w2_hi", align_bytes=64)
+        z_tiles = z_pairs[:].rearrange("p (u j e) -> p u e j", u=2, e=2)
+
+        def look_up(t):
+            nc.vector.tensor_copy(out=looked_up[t][:], in_=y[t][:].indirect(n1_sb[:]))
+
+        def make_z(t):
+            nc.vector.tensor_tensor(out=larger[t][:], in0=looked_up[t][:], in1=y[t][:, :S], op=ALU.max)
+            nc.scalar.activation(out=z_tiles[:, t // 2, t % 2, :], in_=larger[t][:], func=ACT.Copy, scale=gn_sb[:, t : t + 1])
+
+        look_up(0)
+        for t in range(1, PACK):
+            look_up(t)
+            make_z(t - 1)
+        make_z(PACK - 1)
 
         z_bf = sb.tile([P, PACK * S], BF16, name="z_bf", align_bytes=64)
         nc.scalar.copy(
-            out=z_bf[:].rearrange("p (c i t) -> p c t i", i=4, t=PACK),
-            in_=z_planes[:].rearrange("p t (c i) -> p c t i", i=4),
+            out=z_bf[:].bitcast(U32).rearrange("p (j u) -> p j u", u=2),
+            in_=z_pairs[:].bitcast(U32).rearrange("p (u j) -> p j u", u=2),
         )
-        for t in (2, 3):
-            nc.scalar.activation(out=th[t][:], in_=y[t][:, :S], func=ACT.Tanh)
 
-        prod = [sb.tile([P, S], F32, name="prod%d" % t) for t in range(PACK)]
+        tanh_late = sb.tile([P, 2, S], F32, name="tanh_late", tag="after_w2_hi", align_bytes=64)
+        for t in range(2, PACK):
+            tanh_y.append(tanh_late[:, t - 2, :])
+            nc.scalar.activation(out=tanh_y[t], in_=y[t][:, :S], func=ACT.Tanh)
 
-        def product(t):
-            nc.vector.tensor_tensor(out=prod[t][:], in0=y[t][:].indirect(n3_sb[:]), in1=th[t][:], op=ALU.mult)
+        skip = []
 
-        product(0)
-        product(1)
-        w2_codes = sb.tile([P, C], U32, name="w2_codes", align_bytes=64)
+        def make_skip(t, dst):
+            nc.vector.tensor_tensor(out=dst, in0=y[t][:].indirect(n3_sb[:]), in1=tanh_y[t], op=ALU.mult)
+            skip.append(dst)
+
+        skip_early = sb.tile([P, 2, S], F32, name="skip_early", tag="after_xs", align_bytes=64)
+        for t in range(2):
+            make_skip(t, skip_early[:, t, :])
+        w2_codes = sb.tile([P, C], U32, name="w2_codes", tag="after_larger3", align_bytes=64)
         w2_scales = sb.tile([P, C], U8, name="w2_scales", align_bytes=64)
         nc.vector.quantize_mx(out=w2_codes[:].bitcast(FP8X4), scales=w2_scales[:], in_=w2_bf[:])
         z_codes = sb.tile([P, S], U32, name="z_codes", align_bytes=64)
         z_scales = sb.tile([P, S], U8, name="z_scales", align_bytes=64)
         nc.vector.quantize_mx(out=z_codes[:].bitcast(FP8X4), scales=z_scales[:], in_=z_bf[:])
-        product(2)
-        product(3)
+        skip_late = sb.tile([P, 2, S], F32, name="skip_late", align_bytes=64)
+        for t in range(2, PACK):
+            make_skip(t, skip_late[:, t - 2, :])
+
+        for t in range(PACK):
+            h_ps = psum.tile([P, S], F32, name="h_ps", tag="bank%d" % (len(y_pieces) - PACK + t))
+            product_tile(nc, h_ps[:], w2_codes, w2_scales, t, z_codes[:], z_scales[:])
+            nc.scalar.copy(out=h[t][:, :S], in_=h_ps[:])
 
         out_rows = out.rearrange("(p t) c -> p t c", t=PACK)
         for t in range(PACK):
-            acc = psum.tile([P, S], F32, name="h_ps", tag="bank%d" % (2 * t))
-            nc.tensor.matmul_mx(
-                out=acc[:],
-                lhsT=w2_codes[:, P * t : P * (t + 1)].bitcast(FP8X4),
-                lhsT_scale=w2_scales[:, P * t : P * (t + 1)],
-                rhs=z_codes[:].bitcast(FP8X4),
-                rhs_scale=z_scales[:],
-                start=True,
-                stop=True,
-            )
-            nc.scalar.copy(out=h[t][:, :S], in_=acc[:])
-        for t in range(PACK):
-            res = sb.tile([P, S], F32, name="res%d" % t)
-            nc.vector.tensor_tensor(out=res[:], in0=h[t][:].indirect(n2_sb[:]), in1=prod[t][:], op=ALU.subtract)
-            nc.sync.dma_start(out=out_rows[:, t, :], in_=res[:])
+            result = sb.tile([P, S], F32, name="result%d" % t)
+            edges = FINE_EDGES if t == PACK - 1 else [0, S]
+            for c0, c1 in zip(edges[:-1], edges[1:]):
+                picks = n2_sb[:, c0 // GROUP : c1 // GROUP]
+                nc.vector.tensor_tensor(out=result[:, c0:c1], in0=h[t][:].indirect(picks), in1=skip[t][:, c0:c1], op=ALU.subtract)
+                nc.sync.dma_start(out=out_rows[:, t, c0:c1], in_=result[:, c0:c1])

from contextlib import ExitStack

import concourse.mybir as mybir

F32 = mybir.dt.float32
BF16 = mybir.dt.bfloat16
I32 = mybir.dt.int32
U32 = mybir.dt.uint32
U16 = mybir.dt.uint16
U8 = mybir.dt.uint8
FP8X4 = mybir.dt.float8_e4m3fn_x4
ALU = mybir.AluOpType
ACT = mybir.ActivationFunctionType

P = 128
PACK = 4
T = 2048
S = 512
C = 512
GROUP = 16
QUADRANT = 32
HALF = S // 2
WINDOW = 2 * S
FINE_EDGES = [0, HALF, HALF + P, S]
W1_M_SCALAR = 72
FLOPS = 2 * 2 * 512 * 512 * 512


def deal_views(grouped, raw, m0, m1, raw_m0):
    dst = grouped[:].rearrange("p (t m j) -> p m j t", t=PACK, j=PACK)[:, m0:m1]
    src = raw[:].rearrange("p j (m t) -> p m j t", t=PACK)[:, m0 - raw_m0 : m1 - raw_m0]
    return dst, src


def product_tile(nc, acc, w_codes, w_scales, t, codes, scales):
    nc.tensor.matmul_mx(
        out=acc,
        lhsT=w_codes[:, P * t : P * (t + 1)].bitcast(FP8X4),
        lhsT_scale=w_scales[:, P * t : P * (t + 1)],
        rhs=codes.bitcast(FP8X4),
        rhs_scale=scales,
        start=True,
        stop=True,
    )


def tile_picked_skipsoftbbig_none_p_kernel(tc, x_words, x_scales, w1, gn, w2, offs, n1, n2, n3, out):
    nc = tc.nc
    with ExitStack() as ctx:
        lists = ctx.enter_context(tc.tile_pool(name="lists", bufs=1))
        sb = ctx.enter_context(tc.tile_pool(name="sb", bufs=1))
        psum = ctx.enter_context(tc.psum_pool(name="psum", bufs=1))

        offs_sb = lists.tile([P, S // GROUP], U16, name="offs_sb")
        n1_sb = lists.tile([P, S // GROUP], U16, name="n1_sb")
        n2_sb = lists.tile([P, S // GROUP], U16, name="n2_sb")
        n3_sb = lists.tile([P, S // GROUP], U16, name="n3_sb")

        xw = sb.tile([P, T], U32, name="xw", align_bytes=64)
        xs = sb.tile([P, T], U8, name="xs", tag="after_xs", align_bytes=64)
        w1_raw = sb.tile([P, PACK, C], F32, name="w1_raw", align_bytes=64)
        w2_lo = sb.tile([P, PACK, C // 2], F32, name="w2_lo", align_bytes=64)
        w2_hi = sb.tile([P, PACK, C // 2], F32, name="w2_hi", tag="after_w2_hi", align_bytes=64)
        gn_sb = sb.tile([P, PACK], F32, name="gn_sb")
        y = [sb.tile([P, WINDOW], F32, name="y%d" % t, align_bytes=64) for t in range(PACK)]
        h = [sb.tile([P, S if t == PACK - 1 else WINDOW], F32, name="h%d" % t, align_bytes=64) for t in range(PACK)]

        nc.gpsimd.memset(xs[:, : T // 2].bitcast(I32), 0)
        nc.vector.memset(xs[:, T // 2 :].bitcast(I32), 0)

        nc.sync.dma_start(out=w1_raw[:], in_=w1.rearrange("(p j) c -> p j c", j=PACK))
        nc.sync.dma_start(offs_sb[:], offs)
        nc.sync.dma_start(n1_sb[:], n1)
        for q in range(P // QUADRANT):
            nc.sync.dma_start(
                out=xs[QUADRANT * q : QUADRANT * q + 4, :].bitcast(I32),
                in_=x_scales[0, 4 * q : 4 * q + 4, :].bitcast(I32),
            )
        nc.sync.dma_start(out=xw[:].bitcast(I32), in_=x_words[0].rearrange("p n t -> p (n t)").bitcast(I32))
        w2_rows = w2.rearrange("(p j) c -> p j c", j=PACK)
        nc.sync.dma_start(out=w2_lo[:], in_=w2_rows[:, :, : C // 2])
        nc.sync.dma_start(out=w2_hi[:], in_=w2_rows[:, :, C // 2 :])
        nc.sync.dma_start(n3_sb[:], n3)
        nc.sync.dma_start(n2_sb[:], n2)
        nc.sync.dma_start(out=gn_sb[:], in_=gn.rearrange("(p t) o -> p (t o)", t=PACK))

        gs = sb.tile([P, S], U8, name="gs", tag="after_gs", align_bytes=64)
        nc.vector.tensor_copy(out=gs[:], in_=xs[:].indirect(offs_sb[:]))

        w1_bf = sb.tile([P, PACK * C], BF16, name="w1_bf", align_bytes=64)
        dst, src = deal_views(w1_bf, w1_raw, 0, W1_M_SCALAR, 0)
        nc.scalar.copy(out=dst, in_=src)
        dst, src = deal_views(w1_bf, w1_raw, W1_M_SCALAR, P, 0)
        nc.vector.tensor_copy(out=dst, in_=src)
        w1_codes = sb.tile([P, C], U32, name="w1_codes", tag="after_xs", align_bytes=64)
        w1_scales = sb.tile([P, C], U8, name="w1_scales", tag="after_w1_scales", align_bytes=64)
        nc.vector.quantize_mx(out=w1_codes[:].bitcast(FP8X4), scales=w1_scales[:], in_=w1_bf[:])

        gw = sb.tile([P, S], U32, name="gw", tag="after_gw", align_bytes=64)
        for c0 in (0, HALF):
            picks = offs_sb[:, c0 // GROUP : (c0 + HALF) // GROUP]
            nc.vector.tensor_copy(out=gw[:, c0 : c0 + HALF], in_=xw[:].indirect(picks))

        w2_bf = sb.tile([P, PACK * C], BF16, name="w2_bf", align_bytes=64)
        dst, src = deal_views(w2_bf, w2_lo, 0, P // 2, 0)
        nc.vector.tensor_copy(out=dst, in_=src)

        y_pieces = [(0, c0, c1) for c0, c1 in zip(FINE_EDGES[:-1], FINE_EDGES[1:])] + [(t, 0, S) for t in range(1, PACK)]
        for bank, (t, c0, c1) in enumerate(y_pieces):
            y_ps = psum.tile([P, c1 - c0], F32, name="y_ps", tag="bank%d" % bank)
            product_tile(nc, y_ps[:], w1_codes, w1_scales, t, gw[:, c0:c1], gs[:, c0:c1])
            nc.scalar.copy(out=y[t][:, c0:c1], in_=y_ps[:])

        tanh_early = sb.tile([P, 2, S], F32, name="tanh_early", tag="after_gs", align_bytes=64)
        tanh_y = [tanh_early[:, t, :] for t in range(2)]
        for t in range(2):
            nc.scalar.activation(out=tanh_y[t], in_=y[t][:, :S], func=ACT.Tanh)

        for m0 in range(P // 2, P, P // 4):
            dst, src = deal_views(w2_bf, w2_hi, m0, m0 + P // 4, P // 2)
            nc.scalar.copy(out=dst, in_=src)

        looked_up = [sb.tile([P, S], F32, name="looked_up%d" % t, align_bytes=64) for t in range(PACK)]
        larger_tags = ["after_w1_scales", "after_xs", "after_gw", "after_larger3"]
        larger = [sb.tile([P, S], F32, name="larger%d" % t, tag=larger_tags[t], align_bytes=64) for t in range(PACK)]
        z_pairs = sb.tile([P, PACK * S], BF16, name="z_pairs", tag="after_w2_hi", align_bytes=64)
        z_tiles = z_pairs[:].rearrange("p (u j e) -> p u e j", u=2, e=2)

        def look_up(t):
            nc.vector.tensor_copy(out=looked_up[t][:], in_=y[t][:].indirect(n1_sb[:]))

        def make_z(t):
            nc.vector.tensor_tensor(out=larger[t][:], in0=looked_up[t][:], in1=y[t][:, :S], op=ALU.max)
            nc.scalar.activation(out=z_tiles[:, t // 2, t % 2, :], in_=larger[t][:], func=ACT.Copy, scale=gn_sb[:, t : t + 1])

        look_up(0)
        for t in range(1, PACK):
            look_up(t)
            make_z(t - 1)
        make_z(PACK - 1)

        z_bf = sb.tile([P, PACK * S], BF16, name="z_bf", align_bytes=64)
        nc.scalar.copy(
            out=z_bf[:].bitcast(U32).rearrange("p (j u) -> p j u", u=2),
            in_=z_pairs[:].bitcast(U32).rearrange("p (u j) -> p j u", u=2),
        )

        tanh_late = sb.tile([P, 2, S], F32, name="tanh_late", tag="after_w2_hi", align_bytes=64)
        for t in range(2, PACK):
            tanh_y.append(tanh_late[:, t - 2, :])
            nc.scalar.activation(out=tanh_y[t], in_=y[t][:, :S], func=ACT.Tanh)

        skip = []

        def make_skip(t, dst):
            nc.vector.tensor_tensor(out=dst, in0=y[t][:].indirect(n3_sb[:]), in1=tanh_y[t], op=ALU.mult)
            skip.append(dst)

        skip_early = sb.tile([P, 2, S], F32, name="skip_early", tag="after_xs", align_bytes=64)
        for t in range(2):
            make_skip(t, skip_early[:, t, :])
        w2_codes = sb.tile([P, C], U32, name="w2_codes", tag="after_larger3", align_bytes=64)
        w2_scales = sb.tile([P, C], U8, name="w2_scales", align_bytes=64)
        nc.vector.quantize_mx(out=w2_codes[:].bitcast(FP8X4), scales=w2_scales[:], in_=w2_bf[:])
        z_codes = sb.tile([P, S], U32, name="z_codes", align_bytes=64)
        z_scales = sb.tile([P, S], U8, name="z_scales", align_bytes=64)
        nc.vector.quantize_mx(out=z_codes[:].bitcast(FP8X4), scales=z_scales[:], in_=z_bf[:])
        skip_late = sb.tile([P, 2, S], F32, name="skip_late", align_bytes=64)
        for t in range(2, PACK):
            make_skip(t, skip_late[:, t - 2, :])

        for t in range(PACK):
            h_ps = psum.tile([P, S], F32, name="h_ps", tag="bank%d" % (len(y_pieces) - PACK + t))
            product_tile(nc, h_ps[:], w2_codes, w2_scales, t, z_codes[:], z_scales[:])
            nc.scalar.copy(out=h[t][:, :S], in_=h_ps[:])

        out_rows = out.rearrange("(p t) c -> p t c", t=PACK)
        for t in range(PACK):
            result = sb.tile([P, S], F32, name="result%d" % t)
            edges = FINE_EDGES if t == PACK - 1 else [0, S]
            for c0, c1 in zip(edges[:-1], edges[1:]):
                picks = n2_sb[:, c0 // GROUP : c1 // GROUP]
                nc.vector.tensor_tensor(out=result[:, c0:c1], in0=h[t][:].indirect(picks), in1=skip[t][:, c0:c1], op=ALU.subtract)
                nc.sync.dma_start(out=out_rows[:, t, c0:c1], in_=result[:, c0:c1])
